import numpy as np
import ml_dtypes


def mxq(x, axis, fmt="e4m3"):
    dtype, down = {"e4m3": (ml_dtypes.float8_e4m3fn, 7), "e5m2": (ml_dtypes.float8_e5m2, 14)}[fmt]
    v = np.moveaxis(np.asarray(x, np.float32).astype(ml_dtypes.bfloat16).astype(np.float64), axis, -1)
    blocks = v.reshape(v.shape[:-1] + (-1, 32))
    amax = np.abs(blocks).max(-1, keepdims=True)
    byte = np.maximum(np.where(amax > 0, np.frexp(amax)[1] - 1 + 127, 0) - down, 1)
    scale = np.exp2(byte - 127.0)
    codes = (blocks / scale).astype(np.float32).astype(dtype).astype(np.float64)
    return np.moveaxis((codes * scale).reshape(v.shape), -1, axis)


WIDE = False


def mx_kscale(k):
    if not WIDE:
        return np.ones(k)
    levels = np.array([10, -10, 5, -5, 0])
    if k % 512:
        return np.exp2(np.random.permutation(np.resize(levels, k // 32))).repeat(32)
    a = np.empty((k // 512, 16))
    for p in range(k // 512):
        a[p, :8] = np.random.permutation(np.resize(levels, 8))
        for g in range(8):
            far = levels[np.abs(levels - a[p, g]) >= 10]
            a[p, g + 8] = far[np.random.randint(len(far))]
    return np.exp2(a.ravel()).repeat(32)


BF16 = ml_dtypes.bfloat16


def bf(x):
    return np.asarray(x, np.float32).astype(BF16)


def f64(x):
    return np.asarray(x).astype(np.float64)


E2M1 = np.array([0.0, 0.5, 1.0, 1.5, 2.0, 3.0, 4.0, 6.0, -0.0, -0.5, -1.0, -1.5, -2.0, -3.0, -4.0, -6.0])


def pack_weight(w, fmt):
    k, n = w.shape
    w = f64(bf(w)).reshape(k // 32, 32, n)
    amax = np.abs(w).max(1)
    if fmt == "e4m3":
        byte = np.frexp(amax)[1] - 1 + 127 - 7
    else:
        mant, ex = np.frexp(amax / 6.0)
        byte = np.where(mant > 0.5, ex, ex - 1) + 127
    byte = np.clip(np.where(amax > 0, byte, 1), 1, 254)
    scaled = (w * np.exp2(127.0 - byte)[:, None, :]).reshape(k, n).astype(np.float32)
    by_word = np.ascontiguousarray(scaled.reshape(k // 512, 128, 4, n).transpose(0, 1, 3, 2))
    if fmt == "e4m3":
        words = by_word.astype(ml_dtypes.float8_e4m3fn).view(np.uint8)
    else:
        c = by_word.astype(ml_dtypes.float4_e2m1fn).view(np.uint8) & 0xF
        words = c[..., 0::2] | (c[..., 1::2] << 4)
    return np.ascontiguousarray(words), np.ascontiguousarray(byte.astype(np.uint8).reshape(k // 512, 16, n))


def unpack_weight(words, scales, fmt):
    g, p, n, _ = words.shape
    if fmt == "e4m3":
        vals = np.ascontiguousarray(words).view(ml_dtypes.float8_e4m3fn).astype(np.float64)
    else:
        nib = np.empty((g, p, n, 4), np.uint8)
        nib[..., 0::2] = words & 0xF
        nib[..., 1::2] = words >> 4
        vals = E2M1[nib]
    vals = vals * np.repeat(np.exp2(scales.astype(np.float64) - 127.0), 8, axis=1)[..., None]
    return vals.transpose(0, 1, 3, 2).reshape(g * 512, n)

E4M3FN = np.array([(-1.0 if i & 128 else 1.0) * ((1.0 + (i & 7) / 8.0) * 2.0 ** (((i >> 3) & 15) - 7) if i & 120 else (i & 7) * 2.0 ** -9) for i in range(256)])


def e4m3fn_bytes(y):
    return np.clip(np.asarray(y, np.float64), -448.0, 448.0).astype(np.float32).astype(ml_dtypes.float8_e4m3fn).view(np.uint8)


def e4m3fn_values(b):
    return E4M3FN[b]


N, L, R, H = 1024, 512, 1024, 1024


def draw0():
    s, t = mx_kscale(L), mx_kscale(R)
    x = bf(np.random.standard_normal((N, L)) * s)
    k1_words, k1_scales = pack_weight(np.random.standard_normal((L, H)) / np.sqrt(L) / s[:, None], "e4m3")
    u_words, u_scales = pack_weight(np.random.standard_normal((L, R)) / np.sqrt(L) / s[:, None] * t, "e4m3")
    v_words, v_scales = pack_weight(np.random.standard_normal((L, R)) / np.sqrt(L) / s[:, None], "e4m3")
    c_words, c_scales = pack_weight(np.random.standard_normal((R, H)) / np.sqrt(R) / t[:, None], "e4m3")
    return {
        "x": x,
        "k1_words": k1_words,
        "k1_scales": k1_scales,
        "u_words": u_words,
        "u_scales": u_scales,
        "v_words": v_words,
        "v_scales": v_scales,
        "c_words": c_words,
        "c_scales": c_scales,
        "h0": bf(0.4 * np.random.standard_normal(H)),
    }


def core(x, k1_words, k1_scales, u_words, u_scales, v_words, v_scales, c_words, c_scales, h0):
    xq = mxq(f64(x), 1, "e4m3")
    a = xq @ unpack_weight(u_words, u_scales, "e4m3")
    b = xq @ unpack_weight(v_words, v_scales, "e4m3")
    q = a * b
    quad = mxq(q, 1, "e4m3") @ unpack_weight(c_words, c_scales, "e4m3")
    lin = xq @ unpack_weight(k1_words, k1_scales, "e4m3")
    return f64(h0)[None, :] + lin + quad


def setup_inputs():
    drawn = draw0()
    full = np.asarray(drawn['x']).astype(np.float64)
    scale = (np.abs(full).reshape(1024, 4, 128).max(axis=(2,)) / 448.0).astype(np.float32)
    given = {}
    for key, value in drawn.items():
        if key == 'x':
            given['x_bytes'] = e4m3fn_bytes(full / np.repeat(scale.astype(np.float64), 128, axis=1))
            given['x_scale'] = scale
        else:
            given[key] = value
    return given


def reference(x_bytes, x_scale, k1_words, k1_scales, u_words, u_scales, v_words, v_scales, c_words, c_scales, h0):
    return core(e4m3fn_values(x_bytes) * np.repeat(x_scale.astype(np.float64), 128, axis=1), k1_words, k1_scales, u_words, u_scales, v_words, v_scales, c_words, c_scales, h0)

@@ -1,0 +1,298 @@
+from contextlib import ExitStack
+
+import concourse.mybir as mybir
+from concourse.masks import make_identity
+
+N, L, R, H = 1024, 512, 1024, 1024
+FLOPS = 2 * N * (3 * L * 1024 + R * H)
+
+F32 = mybir.dt.float32
+BF16 = mybir.dt.bfloat16
+I32 = mybir.dt.int32
+U32 = mybir.dt.uint32
+U8 = mybir.dt.uint8
+FP8 = mybir.dt.float8_e4m3fn
+FP8X4 = mybir.dt.float8_e4m3fn_x4
+MULT = mybir.AluOpType.mult
+ADD = mybir.AluOpType.add
+COPY = mybir.ActivationFunctionType.Copy
+
+P = 128
+TILES = N // P
+LAG = 2
+WARM = 4
+
+
+def words_view(w, g):
+    return w[g].rearrange("p n t -> p (n t)").bitcast(I32)
+
+
+def tile_lowranksecondordervolterraforecaster_d1p_kernel(
+    tc, x_bytes, x_scale, k1_words, k1_scales, u_words, u_scales, v_words, v_scales, c_words, c_scales, h0, out
+):
+    nc = tc.nc
+    with ExitStack() as ctx:
+        keep = ctx.enter_context(tc.tile_pool(name="keep", bufs=1))
+        work = ctx.enter_context(tc.tile_pool(name="work", bufs=3))
+        psum = ctx.enter_context(tc.psum_pool(name="psum", bufs=1))
+
+        ident = keep.tile([P, P], F32, name="ident")
+        warm = keep.tile([P, 512], BF16, name="warm")
+        h0_all = keep.tile([P, H], BF16, name="h0_all")
+        xb = keep.tile([P, TILES, L], U8, name="xb", align_bytes=64)
+        xs = keep.tile([P, TILES, 4], F32, name="xs")
+        xw = keep.tile([P, TILES, L], BF16, name="xw", align_bytes=64)
+        xq = keep.tile([P, N], U32, name="xq", align_bytes=256)
+        xq_s = keep.tile([P, N], U8, name="xq_s", align_bytes=256)
+        raw = keep.tile([P, 2, R], U32, name="raw", align_bytes=256)
+        raw_us = keep.tile([P, R], U8, name="raw_us", align_bytes=256)
+        raw_vs = keep.tile([P, R], U8, name="raw_vs", align_bytes=256)
+        raw_s = (raw_us, raw_vs)
+        uv = keep.tile([P, 2, R], U32, name="uv", align_bytes=256)
+        uv_s = keep.tile([P, 2, R], U8, name="uv_s", align_bytes=256)
+        k1 = keep.tile([P, H], U32, name="k1", align_bytes=256)
+        kc_s = keep.tile([P, H], U8, name="kc_s", align_bytes=256)
+        cw = keep.tile([P, 2, H], U32, name="cw", align_bytes=256)
+
+        xb_hbm = x_bytes.rearrange("(p j) k -> p j k", j=TILES)
+        xs_hbm = x_scale.rearrange("(p j) b -> p j b", j=TILES)
+        out_hbm = out.rearrange("(p j) h -> p j h", j=TILES)
+
+        def load_scales(queue, tile, row, src):
+            for q in range(4):
+                queue.dma_start(
+                    out=tile[32 * q + row : 32 * q + row + 4 * src.shape[0], :].bitcast(I32),
+                    in_=src[:, 4 * q : 4 * q + 4, :].bitcast(I32),
+                )
+
+        def spread_scales(queue, tile, src):
+            for q in range(4):
+                rows = src[0, 4 * q : 4 * q + 4, :].bitcast(I32)
+                queue.dma_start(
+                    out=tile[32 * q : 32 * q + 32, :].bitcast(I32), in_=rows.unsqueeze(0).to_broadcast([8, 4, R // 4])
+                )
+
+        with tc.manual_schedule():
+            nc.vector.memset(warm[:], 1.0)
+            nc.vector.memset(kc_s[:].bitcast(I32), 0)
+            make_identity(nc, ident[:])
+
+            def load_words(queue, i, g, src):
+                cols = slice(512 * g, 512 * g + 512)
+                queue.dma_start(out=raw[:, i, cols].bitcast(I32), in_=words_view(src, 0)[:, cols])
+
+            def load_x(queue, j0, j1):
+                queue.dma_start(out=xb[:, j0:j1, :], in_=xb_hbm[:, j0:j1, :])
+
+            load_x(nc.sync, 0, 4)
+            nc.sync.dma_start(out=xs[:], in_=xs_hbm)
+            spread_scales(nc.scalar, raw_us, u_scales)
+            load_words(nc.sync, 0, 0, u_words)
+            load_words(nc.sync, 1, 0, v_words)
+            load_words(nc.gpsimd, 0, 1, u_words)
+            load_words(nc.gpsimd, 1, 1, v_words)
+            nc.gpsimd.dma_start(out=h0_all[:], in_=h0.partition_broadcast(P))
+            spread_scales(nc.sync, raw_vs, v_scales)
+            load_x(nc.sync, 4, 8)
+            load_scales(nc.sync, kc_s, 0, k1_scales)
+            nc.sync.dma_start(out=k1[:].bitcast(I32), in_=words_view(k1_words, 0))
+            load_scales(nc.sync, kc_s, 4, c_scales)
+            nc.sync.dma_start(out=cw[:, 0, :].bitcast(I32), in_=words_view(c_words, 0))
+            nc.sync.dma_start(out=cw[:, 1, :].bitcast(I32), in_=words_view(c_words, 1))
+
+            for i in range(WARM):
+                o = psum.tile([P, 512], F32, name="po", bufs=3)
+                nc.tensor.matmul(o[:], lhsT=warm[:, 0:P], rhs=warm[:], start=True, stop=True)
+
+            def widen(j, b, engine):
+                src = xb[:, j, P * b : P * b + P].bitcast(FP8)
+                dst = xw[:, j, P * b : P * b + P]
+                s = xs[:, j, b : b + 1]
+                if engine == "v":
+                    nc.vector.tensor_scalar(out=dst, in0=src, scalar1=s, scalar2=None, op0=MULT)
+                else:
+                    nc.scalar.activation(out=dst, in_=src, func=COPY, scale=s)
+
+            xg_of = {}
+
+            def turn(j0, n, tag="xt", bufs=1):
+                xt = psum.tile([P, n, 2, P], F32, name=tag, bufs=bufs)
+                for i in range(n):
+                    w = xw[:, j0 + i, :].bitcast(F32)
+                    for h in range(2):
+                        nc.tensor.transpose(xt[:, i, h, :], w[:, h::2], ident[:])
+                return xt
+
+            def unload_x(j0, n, xt, engine):
+                xg = work.tile([P, n * L], BF16, name="xg", align_bytes=64, bufs=3)
+                xg_of[j0] = xg
+                dst = xg[:].bitcast(F32).rearrange("p (i m h) -> p i m h", i=n, h=2)
+                src = xt[:].rearrange("p i h m -> p i m h")
+                if engine == "v":
+                    nc.vector.tensor_copy(out=dst, in_=src)
+                else:
+                    nc.scalar.copy(out=dst, in_=src)
+
+            def quant_x(j0, n):
+                c0 = P * j0
+                c1 = P * (j0 + n)
+                nc.vector.quantize_mx(out=xq[:, c0:c1].bitcast(FP8X4), scales=xq_s[:, c0:c1], in_=xg_of[j0][:])
+
+            def permute_scales(i, g):
+                cols = slice(512 * g, 512 * g + 512)
+                nc.vector.tensor_copy(
+                    out=uv_s[:, i, cols].rearrange("p (t m) -> p t m", t=4),
+                    in_=raw_s[i][:, cols].rearrange("p (m t) -> p t m", t=4),
+                )
+
+            def permute_words(i, g):
+                cols = slice(512 * g, 512 * g + 512)
+                nc.vector.tensor_copy(
+                    out=uv[:, i, cols].bitcast(I32).rearrange("p (t m) -> p t m", t=4),
+                    in_=raw[:, i, cols].bitcast(I32).rearrange("p (m t) -> p t m", t=4),
+                )
+
+            ab_of = {}
+            a_of = {}
+            qg_of = {}
+            qc_of = {}
+            o_of = {}
+
+            def stage1(j, g):
+                tok = slice(P * j, P * j + P)
+                for i, nm in enumerate(("pa", "pb")):
+                    bank = psum.tile([P, 4, P], F32, name=nm, bufs=2)
+                    for t in range(4):
+                        c = slice(512 * g + P * t, 512 * g + P * t + P)
+                        nc.tensor.matmul_mx(
+                            out=bank[:, t, :],
+                            lhsT=uv[:, i, c].bitcast(FP8X4),
+                            lhsT_scale=uv_s[:, i, c],
+                            rhs=xq[:, tok].bitcast(FP8X4),
+                            rhs_scale=xq_s[:, tok],
+                            start=True,
+                            stop=True,
+                        )
+                    ab_of[(j, g, i)] = bank
+
+            def copy_a(j, g):
+                a = work.tile([P, P, 4], F32, name="a_sb", bufs=3)
+                nc.scalar.copy(out=a[:], in_=ab_of[(j, g, 0)][:].rearrange("p t n -> p n t"))
+                a_of[(j, g)] = a
+
+            def mult(j, g):
+                if g == 0:
+                    qg_of[j] = work.tile([P, 2, P, 4], BF16, name="qg", align_bytes=64, bufs=3)
+                nc.vector.tensor_tensor(
+                    out=qg_of[j][:, g],
+                    in0=ab_of[(j, g, 1)][:].rearrange("p t n -> p n t"),
+                    in1=a_of[(j, g)][:],
+                    op=MULT,
+                )
+
+            def quant_q(j):
+                qc = work.tile([P, 2 * P], U32, name="qc", align_bytes=256, bufs=4)
+                qs = work.tile([P, 2 * P], U8, name="qs", align_bytes=256, bufs=4)
+                nc.vector.quantize_mx(
+                    out=qc[:].bitcast(FP8X4), scales=qs[:], in_=qg_of[j][:].rearrange("p g n t -> p (g n t)")
+                )
+                qc_of[j] = (qc, qs)
+
+            def linear(j, h):
+                tok = slice(P * j, P * j + P)
+                cols = slice(512 * h, 512 * h + 512)
+                o = psum.tile([P, 512], F32, name="po", bufs=3)
+                nc.tensor.matmul_mx(
+                    out=o[:], lhsT=xq[:, tok].bitcast(FP8X4), lhsT_scale=xq_s[:, tok],
+                    rhs=k1[:, cols].bitcast(FP8X4), rhs_scale=kc_s[:, cols], start=True, stop=False,
+                )
+                o_of[(j, h)] = o
+
+            def quadratic(j, h):
+                cols = slice(512 * h, 512 * h + 512)
+                qc, qs = qc_of[j]
+                o = o_of[(j, h)]
+                for g in range(2):
+                    r = slice(P * g, P * g + P)
+                    nc.tensor.matmul_mx(
+                        out=o[:], lhsT=qc[:, r].bitcast(FP8X4), lhsT_scale=qs[:, r],
+                        rhs=cw[:, g, cols].bitcast(FP8X4), rhs_scale=kc_s[4 + 4 * g :, cols], start=False, stop=(g == 1),
+                    )
+
+            def finish(j, h):
+                cols = slice(512 * h, 512 * h + 512)
+                ob = work.tile([P, 512], F32, name="ob", bufs=4)
+                nc.vector.tensor_tensor(out=ob[:], in0=o_of[(j, h)][:], in1=h0_all[:, cols], op=ADD)
+                nc.sync.dma_start(out=out_hbm[:, j, cols], in_=ob[:])
+
+            for b in range(4):
+                widen(0, b, "v")
+            for j in (1, 2):
+                for b in range(4):
+                    widen(j, b, "s")
+            xt = turn(0, 1)
+            unload_x(0, 1, xt, "s")
+            xt = turn(1, 1, "po", 3)
+            unload_x(1, 1, xt, "s")
+            for b in range(4):
+                widen(3, b, "s")
+            permute_scales(0, 0)
+            permute_words(0, 0)
+            quant_x(0, 1)
+            permute_scales(1, 0)
+            permute_words(1, 0)
+            quant_x(1, 1)
+            permute_words(0, 1)
+            permute_scales(0, 1)
+            permute_words(1, 1)
+            permute_scales(1, 1)
+
+            def unit(j, g):
+                stage1(j, g)
+                copy_a(j, g)
+                mult(j, g)
+
+            stage1(0, 0)
+            xt = turn(2, 2)
+            copy_a(0, 0)
+            mult(0, 0)
+            unload_x(2, 2, xt, "s")
+            unit(0, 1)
+            for b in range(4):
+                widen(4, b, "s")
+            quant_x(2, 2)
+            unit(1, 0)
+            for b in range(4):
+                widen(5, b, "s")
+            quant_q(0)
+            linear(0, 0)
+            unit(1, 1)
+            xt = turn(4, 2)
+            for b in range(4):
+                widen(6, b, "s")
+            unload_x(4, 2, xt, "s")
+            linear(0, 1)
+            quant_q(1)
+
+            for s in range(2, TILES + LAG):
+                j = s
+                e = s - LAG
+                for g in range(2):
+                    if j < TILES:
+                        unit(j, g)
+                    if j == 2:
+                        if g == 0:
+                            for b in range(4):
+                                widen(7, b, "s")
+                            quant_x(4, 2)
+                        else:
+                            xt = turn(6, 2)
+                            unload_x(6, 2, xt, "s")
+                    if j == 3 and g == 0:
+                        quant_x(6, 2)
+                    if e > 0:
+                        linear(e, g)
+                    quadratic(e, g)
+                    finish(e, g)
+                if j < TILES:
+                    quant_q(j)

@@ -20,7 +20,7 @@ COPY = mybir.ActivationFunctionType.Copy
 P = 128
 TILES = N // P
 LAG = 2
-WARM = 4
+WARM = (4, 2, 0)
 
 
 def words_view(w, g):
@@ -38,6 +38,7 @@ def tile_lowranksecondordervolterraforecaster_d1p_kernel(
 
         ident = keep.tile([P, P], F32, name="ident")
         warm = keep.tile([P, 512], BF16, name="warm")
+        h0_row = keep.tile([P, H], BF16, name="h0_row")
         h0_all = keep.tile([P, H], BF16, name="h0_all")
         xb = keep.tile([P, TILES, L], U8, name="xb", align_bytes=64)
         xs = keep.tile([P, TILES, 4], F32, name="xs")
@@ -75,7 +76,7 @@ def tile_lowranksecondordervolterraforecaster_d1p_kernel(
         with tc.manual_schedule():
             nc.vector.memset(warm[:], 1.0)
             nc.vector.memset(kc_s[:].bitcast(I32), 0)
-            make_identity(nc, ident[:])
+            nc.vector.memset(h0_row[:].bitcast(I32), 0)
 
             def load_words(queue, i, g, src):
                 cols = slice(512 * g, 512 * g + 512)
@@ -87,22 +88,26 @@ def tile_lowranksecondordervolterraforecaster_d1p_kernel(
             load_x(nc.sync, 0, 4)
             nc.sync.dma_start(out=xs[:], in_=xs_hbm)
             spread_scales(nc.scalar, raw_us, u_scales)
-            load_words(nc.sync, 0, 0, u_words)
-            load_words(nc.sync, 1, 0, v_words)
+            load_words(nc.gpsimd, 1, 0, v_words)
+            make_identity(nc, ident[:])
             load_words(nc.gpsimd, 0, 1, u_words)
-            load_words(nc.gpsimd, 1, 1, v_words)
-            nc.gpsimd.dma_start(out=h0_all[:], in_=h0.partition_broadcast(P))
+            load_words(nc.sync, 0, 0, u_words)
             spread_scales(nc.sync, raw_vs, v_scales)
+            load_words(nc.sync, 1, 1, v_words)
             load_x(nc.sync, 4, 8)
             load_scales(nc.sync, kc_s, 0, k1_scales)
             nc.sync.dma_start(out=k1[:].bitcast(I32), in_=words_view(k1_words, 0))
+            nc.sync.dma_start(out=h0_row[0:1, :], in_=h0.rearrange("(o h) -> o h", o=1))
             load_scales(nc.sync, kc_s, 4, c_scales)
             nc.sync.dma_start(out=cw[:, 0, :].bitcast(I32), in_=words_view(c_words, 0))
             nc.sync.dma_start(out=cw[:, 1, :].bitcast(I32), in_=words_view(c_words, 1))
 
-            for i in range(WARM):
-                o = psum.tile([P, 512], F32, name="po", bufs=3)
-                nc.tensor.matmul(o[:], lhsT=warm[:, 0:P], rhs=warm[:], start=True, stop=True)
+            def keep_clock(n):
+                for i in range(n):
+                    o = psum.tile([P, 512], F32, name="po", bufs=4)
+                    nc.tensor.matmul(o[:], lhsT=warm[:, 0:P], rhs=warm[:], start=True, stop=True)
+
+            keep_clock(WARM[0])
 
             def widen(j, b, engine):
                 src = xb[:, j, P * b : P * b + P].bitcast(FP8)
@@ -115,8 +120,8 @@ def tile_lowranksecondordervolterraforecaster_d1p_kernel(
 
             xg_of = {}
 
-            def turn(j0, n, tag="xt", bufs=1):
-                xt = psum.tile([P, n, 2, P], F32, name=tag, bufs=bufs)
+            def turn(j0, n):
+                xt = psum.tile([P, n, 2, P], F32, name="po", bufs=4)
                 for i in range(n):
                     w = xw[:, j0 + i, :].bitcast(F32)
                     for h in range(2):
@@ -201,7 +206,7 @@ def tile_lowranksecondordervolterraforecaster_d1p_kernel(
             def linear(j, h):
                 tok = slice(P * j, P * j + P)
                 cols = slice(512 * h, 512 * h + 512)
-                o = psum.tile([P, 512], F32, name="po", bufs=3)
+                o = psum.tile([P, 512], F32, name="po", bufs=4)
                 nc.tensor.matmul_mx(
                     out=o[:], lhsT=xq[:, tok].bitcast(FP8X4), lhsT_scale=xq_s[:, tok],
                     rhs=k1[:, cols].bitcast(FP8X4), rhs_scale=kc_s[:, cols], start=True, stop=False,
@@ -225,6 +230,13 @@ def tile_lowranksecondordervolterraforecaster_d1p_kernel(
                 nc.vector.tensor_tensor(out=ob[:], in0=o_of[(j, h)][:], in1=h0_all[:, cols], op=ADD)
                 nc.sync.dma_start(out=out_hbm[:, j, cols], in_=ob[:])
 
+            def h0_spread():
+                for h in range(2):
+                    cols = slice(512 * h, 512 * h + 512)
+                    o = psum.tile([P, 512], F32, name="po", bufs=4)
+                    nc.tensor.matmul(o[:], lhsT=warm[:, 0:P], rhs=h0_row[:, cols], start=True, stop=True)
+                    nc.vector.tensor_copy(out=h0_all[:, cols], in_=o[:])
+
             for b in range(4):
                 widen(0, b, "v")
             for j in (1, 2):
@@ -232,8 +244,9 @@ def tile_lowranksecondordervolterraforecaster_d1p_kernel(
                     widen(j, b, "s")
             xt = turn(0, 1)
             unload_x(0, 1, xt, "s")
-            xt = turn(1, 1, "po", 3)
+            xt = turn(1, 1)
             unload_x(1, 1, xt, "s")
+            keep_clock(WARM[1])
             for b in range(4):
                 widen(3, b, "s")
             permute_scales(0, 0)
@@ -253,6 +266,7 @@ def tile_lowranksecondordervolterraforecaster_d1p_kernel(
                 mult(j, g)
 
             stage1(0, 0)
+            keep_clock(WARM[2])
             xt = turn(2, 2)
             copy_a(0, 0)
             mult(0, 0)
@@ -267,10 +281,7 @@ def tile_lowranksecondordervolterraforecaster_d1p_kernel(
             quant_q(0)
             linear(0, 0)
             unit(1, 1)
-            xt = turn(4, 2)
-            for b in range(4):
-                widen(6, b, "s")
-            unload_x(4, 2, xt, "s")
+            h0_spread()
             linear(0, 1)
             quant_q(1)
 
@@ -280,16 +291,14 @@ def tile_lowranksecondordervolterraforecaster_d1p_kernel(
                 for g in range(2):
                     if j < TILES:
                         unit(j, g)
-                    if j == 2:
-                        if g == 0:
-                            for b in range(4):
-                                widen(7, b, "s")
-                            quant_x(4, 2)
-                        else:
-                            xt = turn(6, 2)
-                            unload_x(6, 2, xt, "s")
-                    if j == 3 and g == 0:
-                        quant_x(6, 2)
+                    if j == 3 or (j == 4 and g == 0):
+                        for b in range(4 if j == 4 else 2):
+                            widen(j + 3, 2 * g + b, "s")
+                    if j in (2, 4) and g == j // 2 - 1:
+                        xt = turn(j + 2, 2)
+                        unload_x(j + 2, 2, xt, "s")
+                    if (j == 2 and g == 1) or (j == 5 and g == 0):
+                        quant_x(4 if j == 2 else 6, 2)
                     if e > 0:
                         linear(e, g)
                     quadratic(e, g)

@@ -20,7 +20,7 @@ COPY = mybir.ActivationFunctionType.Copy
 P = 128
 TILES = N // P
 LAG = 2
-WARM = (4, 2, 0)
+WARM = (4, 1, 0)
 
 
 def words_view(w, g):
@@ -34,11 +34,10 @@ def tile_lowranksecondordervolterraforecaster_d1p_kernel(
     with ExitStack() as ctx:
         keep = ctx.enter_context(tc.tile_pool(name="keep", bufs=1))
         work = ctx.enter_context(tc.tile_pool(name="work", bufs=3))
-        psum = ctx.enter_context(tc.psum_pool(name="psum", bufs=1))
+        psum = ctx.enter_context(tc.psum_pool(name="psum", bufs=8))
 
         ident = keep.tile([P, P], F32, name="ident")
         warm = keep.tile([P, 512], BF16, name="warm")
-        h0_row = keep.tile([P, H], BF16, name="h0_row")
         h0_all = keep.tile([P, H], BF16, name="h0_all")
         xb = keep.tile([P, TILES, L], U8, name="xb", align_bytes=64)
         xs = keep.tile([P, TILES, 4], F32, name="xs")
@@ -74,9 +73,10 @@ def tile_lowranksecondordervolterraforecaster_d1p_kernel(
                 )
 
         with tc.manual_schedule():
+            nc.vector.memset(ident[:], 0.0)
             nc.vector.memset(warm[:], 1.0)
             nc.vector.memset(kc_s[:].bitcast(I32), 0)
-            nc.vector.memset(h0_row[:].bitcast(I32), 0)
+            make_identity(nc, ident[:], nomemset=True)
 
             def load_words(queue, i, g, src):
                 cols = slice(512 * g, 512 * g + 512)
@@ -88,23 +88,22 @@ def tile_lowranksecondordervolterraforecaster_d1p_kernel(
             load_x(nc.sync, 0, 4)
             nc.sync.dma_start(out=xs[:], in_=xs_hbm)
             spread_scales(nc.scalar, raw_us, u_scales)
-            load_words(nc.gpsimd, 1, 0, v_words)
-            make_identity(nc, ident[:])
-            load_words(nc.gpsimd, 0, 1, u_words)
             load_words(nc.sync, 0, 0, u_words)
+            load_words(nc.sync, 1, 0, v_words)
+            load_words(nc.gpsimd, 1, 1, v_words)
             spread_scales(nc.sync, raw_vs, v_scales)
-            load_words(nc.sync, 1, 1, v_words)
+            load_words(nc.sync, 0, 1, u_words)
             load_x(nc.sync, 4, 8)
             load_scales(nc.sync, kc_s, 0, k1_scales)
             nc.sync.dma_start(out=k1[:].bitcast(I32), in_=words_view(k1_words, 0))
-            nc.sync.dma_start(out=h0_row[0:1, :], in_=h0.rearrange("(o h) -> o h", o=1))
             load_scales(nc.sync, kc_s, 4, c_scales)
             nc.sync.dma_start(out=cw[:, 0, :].bitcast(I32), in_=words_view(c_words, 0))
             nc.sync.dma_start(out=cw[:, 1, :].bitcast(I32), in_=words_view(c_words, 1))
+            nc.sync.dma_start(out=h0_all[:], in_=h0.partition_broadcast(P))
 
             def keep_clock(n):
                 for i in range(n):
-                    o = psum.tile([P, 512], F32, name="po", bufs=4)
+                    o = psum.tile([P, 512], F32, name="ps")
                     nc.tensor.matmul(o[:], lhsT=warm[:, 0:P], rhs=warm[:], start=True, stop=True)
 
             keep_clock(WARM[0])
@@ -121,7 +120,7 @@ def tile_lowranksecondordervolterraforecaster_d1p_kernel(
             xg_of = {}
 
             def turn(j0, n):
-                xt = psum.tile([P, n, 2, P], F32, name="po", bufs=4)
+                xt = psum.tile([P, n, 2, P], F32, name="ps")
                 for i in range(n):
                     w = xw[:, j0 + i, :].bitcast(F32)
                     for h in range(2):
@@ -165,8 +164,8 @@ def tile_lowranksecondordervolterraforecaster_d1p_kernel(
 
             def stage1(j, g):
                 tok = slice(P * j, P * j + P)
-                for i, nm in enumerate(("pa", "pb")):
-                    bank = psum.tile([P, 4, P], F32, name=nm, bufs=2)
+                for i in range(2):
+                    bank = psum.tile([P, 4, P], F32, name="ps")
                     for t in range(4):
                         c = slice(512 * g + P * t, 512 * g + P * t + P)
                         nc.tensor.matmul_mx(
@@ -203,20 +202,20 @@ def tile_lowranksecondordervolterraforecaster_d1p_kernel(
                 )
                 qc_of[j] = (qc, qs)
 
-            def linear(j, h):
+            def linear(j, c0, width=512):
                 tok = slice(P * j, P * j + P)
-                cols = slice(512 * h, 512 * h + 512)
-                o = psum.tile([P, 512], F32, name="po", bufs=4)
+                cols = slice(c0, c0 + width)
+                o = psum.tile([P, width], F32, name="ps")
                 nc.tensor.matmul_mx(
                     out=o[:], lhsT=xq[:, tok].bitcast(FP8X4), lhsT_scale=xq_s[:, tok],
                     rhs=k1[:, cols].bitcast(FP8X4), rhs_scale=kc_s[:, cols], start=True, stop=False,
                 )
-                o_of[(j, h)] = o
+                o_of[(j, c0)] = o
 
-            def quadratic(j, h):
-                cols = slice(512 * h, 512 * h + 512)
+            def quadratic(j, c0, width=512):
+                cols = slice(c0, c0 + width)
                 qc, qs = qc_of[j]
-                o = o_of[(j, h)]
+                o = o_of[(j, c0)]
                 for g in range(2):
                     r = slice(P * g, P * g + P)
                     nc.tensor.matmul_mx(
@@ -224,84 +223,102 @@ def tile_lowranksecondordervolterraforecaster_d1p_kernel(
                         rhs=cw[:, g, cols].bitcast(FP8X4), rhs_scale=kc_s[4 + 4 * g :, cols], start=False, stop=(g == 1),
                     )
 
-            def finish(j, h):
-                cols = slice(512 * h, 512 * h + 512)
-                ob = work.tile([P, 512], F32, name="ob", bufs=4)
-                nc.vector.tensor_tensor(out=ob[:], in0=o_of[(j, h)][:], in1=h0_all[:, cols], op=ADD)
+            def finish(j, c0, width=512):
+                cols = slice(c0, c0 + width)
+                ob = work.tile([P, width], F32, name="ob", bufs=4)
+                nc.vector.tensor_tensor(out=ob[:], in0=o_of[(j, c0)][:], in1=h0_all[:, cols], op=ADD)
                 nc.sync.dma_start(out=out_hbm[:, j, cols], in_=ob[:])
 
-            def h0_spread():
-                for h in range(2):
-                    cols = slice(512 * h, 512 * h + 512)
-                    o = psum.tile([P, 512], F32, name="po", bufs=4)
-                    nc.tensor.matmul(o[:], lhsT=warm[:, 0:P], rhs=h0_row[:, cols], start=True, stop=True)
-                    nc.vector.tensor_copy(out=h0_all[:, cols], in_=o[:])
-
-            for b in range(4):
-                widen(0, b, "v")
-            for j in (1, 2):
+            for j in (0, 1):
                 for b in range(4):
-                    widen(j, b, "s")
-            xt = turn(0, 1)
-            unload_x(0, 1, xt, "s")
-            xt = turn(1, 1)
-            unload_x(1, 1, xt, "s")
+                    widen(j, b, "v" if j == 0 else "s")
+            for j in (2, 3):
+                for b in range(4):
+                    widen(j, b, "v" if j == 2 else "s")
+            for j in (0, 1):
+                xt = turn(j, 1)
+                unload_x(j, 1, xt, "s")
+            xt = turn(2, 2)
+            unload_x(2, 2, xt, "s")
             keep_clock(WARM[1])
-            for b in range(4):
-                widen(3, b, "s")
-            permute_scales(0, 0)
             permute_words(0, 0)
-            quant_x(0, 1)
-            permute_scales(1, 0)
             permute_words(1, 0)
+            permute_scales(0, 0)
+            quant_x(0, 1)
             quant_x(1, 1)
-            permute_words(0, 1)
             permute_scales(0, 1)
-            permute_words(1, 1)
+            permute_scales(1, 0)
             permute_scales(1, 1)
+            permute_words(0, 1)
+            permute_words(1, 1)
 
             def unit(j, g):
                 stage1(j, g)
                 copy_a(j, g)
                 mult(j, g)
 
-            stage1(0, 0)
-            keep_clock(WARM[2])
-            xt = turn(2, 2)
-            copy_a(0, 0)
-            mult(0, 0)
-            unload_x(2, 2, xt, "s")
-            unit(0, 1)
-            for b in range(4):
-                widen(4, b, "s")
-            quant_x(2, 2)
+            unit(0, 0)
             unit(1, 0)
-            for b in range(4):
-                widen(5, b, "s")
-            quant_q(0)
-            linear(0, 0)
+            quant_x(2, 2)
+            unit(0, 1)
             unit(1, 1)
-            h0_spread()
-            linear(0, 1)
+            quant_q(0)
+            unit(2, 0)
             quant_q(1)
-
-            for s in range(2, TILES + LAG):
-                j = s
-                e = s - LAG
-                for g in range(2):
-                    if j < TILES:
-                        unit(j, g)
-                    if j == 3 or (j == 4 and g == 0):
-                        for b in range(4 if j == 4 else 2):
-                            widen(j + 3, 2 * g + b, "s")
-                    if j in (2, 4) and g == j // 2 - 1:
-                        xt = turn(j + 2, 2)
-                        unload_x(j + 2, 2, xt, "s")
-                    if (j == 2 and g == 1) or (j == 5 and g == 0):
-                        quant_x(4 if j == 2 else 6, 2)
-                    if e > 0:
-                        linear(e, g)
-                    quadratic(e, g)
-                    finish(e, g)
-                if j < TILES:
-                    quant_q(j)
+            unit(2, 1)
+            linear(0, 0)
+            unit(3, 0)
+            quant_q(2)
+            linear(0, 512)
+            unit(3, 1)
+            for j in (4, 5, 6, 7):
+                for b in range(4):
+                    widen(j, b, "s")
+            for h in range(2):
+                quadratic(0, 512 * h)
+                finish(0, 512 * h)
+                if h == 0:
+                    quant_q(3)
+            for h in range(2):
+                linear(1, 512 * h)
+                quadratic(1, 512 * h)
+                finish(1, 512 * h)
+            xt = turn(4, 2)
+            unload_x(4, 2, xt, "s")
+            for h in range(2):
+                linear(2, 512 * h)
+                quadratic(2, 512 * h)
+                finish(2, 512 * h)
+            quant_x(4, 2)
+            xt = turn(6, 2)
+            unload_x(6, 2, xt, "s")
+            for h in range(2):
+                linear(3, 512 * h)
+                quadratic(3, 512 * h)
+            finish(3, 0)
+            quant_x(6, 2)
+            finish(3, 512)
+            unit(4, 0)
+            unit(4, 1)
+            unit(5, 0)
+            quant_q(4)
+            unit(5, 1)
+            unit(6, 0)
+            quant_q(5)
+            unit(6, 1)
+            linear(4, 0)
+            unit(7, 0)
+            quant_q(6)
+            linear(4, 512)
+            unit(7, 1)
+            for h in range(2):
+                quadratic(4, 512 * h)
+                finish(4, 512 * h)
+                if h == 0:
+                    quant_q(7)
+            for j in (5, 6, 7):
+                for h in range(2):
+                    for c in ((512 * h, 512),) if (j, h) != (7, 1) else ((512, 256), (768, 256)):
+                        linear(j, *c)
+                        quadratic(j, *c)
+                        finish(j, *c)

@@ -65,10 +65,10 @@ def tile_lowranksecondordervolterraforecaster_d1p_kernel(
                     in_=src[:, 4 * q : 4 * q + 4, :].bitcast(I32),
                 )
 
-        def spread_scales(queue, tile, src):
+        def spread_scales(queues, tile, src):
             for q in range(4):
                 rows = src[0, 4 * q : 4 * q + 4, :].bitcast(I32)
-                queue.dma_start(
+                queues[q].dma_start(
                     out=tile[32 * q : 32 * q + 32, :].bitcast(I32), in_=rows.unsqueeze(0).to_broadcast([8, 4, R // 4])
                 )
 
@@ -87,14 +87,14 @@ def tile_lowranksecondordervolterraforecaster_d1p_kernel(
 
             load_x(nc.sync, 0, 4)
             nc.sync.dma_start(out=xs[:], in_=xs_hbm)
-            spread_scales(nc.scalar, raw_us, u_scales)
+            spread_scales((nc.scalar, nc.scalar, nc.sync, nc.sync), raw_us, u_scales)
             load_words(nc.sync, 0, 0, u_words)
             load_words(nc.sync, 1, 0, v_words)
-            load_words(nc.gpsimd, 1, 1, v_words)
-            spread_scales(nc.sync, raw_vs, v_scales)
+            spread_scales((nc.sync,) * 4, raw_vs, v_scales)
             load_words(nc.sync, 0, 1, u_words)
+            load_words(nc.sync, 1, 1, v_words)
+            load_scales(nc.gpsimd, kc_s, 0, k1_scales)
             load_x(nc.sync, 4, 8)
-            load_scales(nc.sync, kc_s, 0, k1_scales)
             nc.sync.dma_start(out=k1[:].bitcast(I32), in_=words_view(k1_words, 0))
             load_scales(nc.sync, kc_s, 4, c_scales)
             nc.sync.dma_start(out=cw[:, 0, :].bitcast(I32), in_=words_view(c_words, 0))
@@ -162,31 +162,25 @@ def tile_lowranksecondordervolterraforecaster_d1p_kernel(
             qc_of = {}
             o_of = {}
 
-            def stage1(j, g):
+            def stage1(j, g, i):
                 tok = slice(P * j, P * j + P)
-                for i in range(2):
-                    bank = psum.tile([P, 4, P], F32, name="ps")
-                    for t in range(4):
-                        c = slice(512 * g + P * t, 512 * g + P * t + P)
-                        nc.tensor.matmul_mx(
-                            out=bank[:, t, :],
-                            lhsT=uv[:, i, c].bitcast(FP8X4),
-                            lhsT_scale=uv_s[:, i, c],
-                            rhs=xq[:, tok].bitcast(FP8X4),
-                            rhs_scale=xq_s[:, tok],
-                            start=True,
-                            stop=True,
-                        )
-                    ab_of[(j, g, i)] = bank
+                bank = psum.tile([P, 4, P], F32, name="ps")
+                for t in range(4):
+                    c = slice(512 * g + P * t, 512 * g + P * t + P)
+                    nc.tensor.matmul_mx(
+                        out=bank[:, t, :], lhsT=uv[:, i, c].bitcast(FP8X4), lhsT_scale=uv_s[:, i, c],
+                        rhs=xq[:, tok].bitcast(FP8X4), rhs_scale=xq_s[:, tok], start=True, stop=True,
+                    )
+                ab_of[(j, g, i)] = bank
 
             def copy_a(j, g):
-                a = work.tile([P, P, 4], F32, name="a_sb", bufs=3)
+                a = work.tile([P, P, 4], F32, name="a_sb", bufs=6)
                 nc.scalar.copy(out=a[:], in_=ab_of[(j, g, 0)][:].rearrange("p t n -> p n t"))
                 a_of[(j, g)] = a
 
             def mult(j, g):
                 if g == 0:
-                    qg_of[j] = work.tile([P, 2, P, 4], BF16, name="qg", align_bytes=64, bufs=3)
+                    qg_of[j] = work.tile([P, 2, P, 4], BF16, name="qg", align_bytes=64, bufs=6)
                 nc.vector.tensor_tensor(
                     out=qg_of[j][:, g],
                     in0=ab_of[(j, g, 1)][:].rearrange("p t n -> p n t"),
@@ -195,8 +189,8 @@ def tile_lowranksecondordervolterraforecaster_d1p_kernel(
                 )
 
             def quant_q(j):
-                qc = work.tile([P, 2 * P], U32, name="qc", align_bytes=256, bufs=4)
-                qs = work.tile([P, 2 * P], U8, name="qs", align_bytes=256, bufs=4)
+                qc = work.tile([P, 2 * P], U32, name="qc", align_bytes=256, bufs=6)
+                qs = work.tile([P, 2 * P], U8, name="qs", align_bytes=256, bufs=6)
                 nc.vector.quantize_mx(
                     out=qc[:].bitcast(FP8X4), scales=qs[:], in_=qg_of[j][:].rearrange("p g n t -> p (g n t)")
                 )
@@ -225,79 +219,89 @@ def tile_lowranksecondordervolterraforecaster_d1p_kernel(
 
             def finish(j, c0, width=512):
                 cols = slice(c0, c0 + width)
-                ob = work.tile([P, width], F32, name="ob", bufs=4)
+                ob = work.tile([P, width], F32, name="ob", bufs=10)
                 nc.vector.tensor_tensor(out=ob[:], in0=o_of[(j, c0)][:], in1=h0_all[:, cols], op=ADD)
                 nc.sync.dma_start(out=out_hbm[:, j, cols], in_=ob[:])
 
-            for j in (0, 1):
+            for j in range(4):
                 for b in range(4):
-                    widen(j, b, "v" if j == 0 else "s")
-            for j in (2, 3):
-                for b in range(4):
-                    widen(j, b, "v" if j == 2 else "s")
+                    widen(j, b, "sv"[j % 2 == 0])
             for j in (0, 1):
                 xt = turn(j, 1)
                 unload_x(j, 1, xt, "s")
             xt = turn(2, 2)
             unload_x(2, 2, xt, "s")
             keep_clock(WARM[1])
+            permute_scales(0, 0)
             permute_words(0, 0)
             permute_words(1, 0)
-            permute_scales(0, 0)
             quant_x(0, 1)
             quant_x(1, 1)
-            permute_scales(0, 1)
             permute_scales(1, 0)
+            permute_scales(0, 1)
             permute_scales(1, 1)
-            permute_words(0, 1)
-            permute_words(1, 1)
-
-            def unit(j, g):
-                stage1(j, g)
-                copy_a(j, g)
-                mult(j, g)
-
-            unit(0, 0)
-            unit(1, 0)
             quant_x(2, 2)
-            unit(0, 1)
-            unit(1, 1)
+            permute_words(0, 1)
+
+            def stage1_pair(j, g):
+                for i in range(2):
+                    for jj in (j, j + 1):
+                        stage1(jj, g, i)
+                        if i == 0:
+                            copy_a(jj, g)
+
+            stage1_pair(0, 0)
+            mult(0, 0)
+            permute_words(1, 1)
+            mult(1, 0)
+            stage1_pair(2, 0)
+            mult(2, 0)
+            mult(3, 0)
+            stage1_pair(0, 1)
+            mult(0, 1)
             quant_q(0)
-            unit(2, 0)
+            mult(1, 1)
+            stage1_pair(2, 1)
+            mult(2, 1)
             quant_q(1)
-            unit(2, 1)
-            linear(0, 0)
-            unit(3, 0)
+            mult(3, 1)
             quant_q(2)
-            linear(0, 512)
-            unit(3, 1)
             for j in (4, 5, 6, 7):
                 for b in range(4):
                     widen(j, b, "s")
+            linear(0, 0)
+            linear(0, 512)
+            linear(1, 0)
             for h in range(2):
                 quadratic(0, 512 * h)
                 finish(0, 512 * h)
                 if h == 0:
                     quant_q(3)
+            linear(1, 512)
             for h in range(2):
-                linear(1, 512 * h)
                 quadratic(1, 512 * h)
                 finish(1, 512 * h)
-            xt = turn(4, 2)
-            unload_x(4, 2, xt, "s")
+            for j in (4, 6):
+                xt = turn(j, 2)
+                unload_x(j, 2, xt, "s")
             for h in range(2):
                 linear(2, 512 * h)
                 quadratic(2, 512 * h)
                 finish(2, 512 * h)
             quant_x(4, 2)
-            xt = turn(6, 2)
-            unload_x(6, 2, xt, "s")
             for h in range(2):
                 linear(3, 512 * h)
                 quadratic(3, 512 * h)
             finish(3, 0)
             quant_x(6, 2)
             finish(3, 512)
+
+            def unit(j, g):
+                stage1(j, g, 0)
+                stage1(j, g, 1)
+                copy_a(j, g)
+                mult(j, g)
+
             unit(4, 0)
             unit(4, 1)
             unit(5, 0)

@@ -20,7 +20,6 @@ COPY = mybir.ActivationFunctionType.Copy
 P = 128
 TILES = N // P
 LAG = 2
-WARM = (4, 1, 0)
 
 
 def words_view(w, g):
@@ -37,7 +36,7 @@ def tile_lowranksecondordervolterraforecaster_d1p_kernel(
         psum = ctx.enter_context(tc.psum_pool(name="psum", bufs=8))
 
         ident = keep.tile([P, P], F32, name="ident")
-        warm = keep.tile([P, 512], BF16, name="warm")
+        ident_pool = keep.tile([P, P], F32, name="ident_pool")
         h0_all = keep.tile([P, H], BF16, name="h0_all")
         xb = keep.tile([P, TILES, L], U8, name="xb", align_bytes=64)
         xs = keep.tile([P, TILES, 4], F32, name="xs")
@@ -73,10 +72,8 @@ def tile_lowranksecondordervolterraforecaster_d1p_kernel(
                 )
 
         with tc.manual_schedule():
-            nc.vector.memset(ident[:], 0.0)
-            nc.vector.memset(warm[:], 1.0)
             nc.vector.memset(kc_s[:].bitcast(I32), 0)
-            make_identity(nc, ident[:], nomemset=True)
+            make_identity(nc, ident_pool[:])
 
             def load_words(queue, i, g, src):
                 cols = slice(512 * g, 512 * g + 512)
@@ -88,12 +85,13 @@ def tile_lowranksecondordervolterraforecaster_d1p_kernel(
             load_x(nc.sync, 0, 4)
             nc.sync.dma_start(out=xs[:], in_=xs_hbm)
             spread_scales((nc.scalar, nc.scalar, nc.sync, nc.sync), raw_us, u_scales)
+            nc.scalar.copy(out=ident[:], in_=ident_pool[:])
             load_words(nc.sync, 0, 0, u_words)
             load_words(nc.sync, 1, 0, v_words)
             spread_scales((nc.sync,) * 4, raw_vs, v_scales)
             load_words(nc.sync, 0, 1, u_words)
             load_words(nc.sync, 1, 1, v_words)
-            load_scales(nc.gpsimd, kc_s, 0, k1_scales)
+            load_scales(nc.sync, kc_s, 0, k1_scales)
             load_x(nc.sync, 4, 8)
             nc.sync.dma_start(out=k1[:].bitcast(I32), in_=words_view(k1_words, 0))
             load_scales(nc.sync, kc_s, 4, c_scales)
@@ -101,12 +99,6 @@ def tile_lowranksecondordervolterraforecaster_d1p_kernel(
             nc.sync.dma_start(out=cw[:, 1, :].bitcast(I32), in_=words_view(c_words, 1))
             nc.sync.dma_start(out=h0_all[:], in_=h0.partition_broadcast(P))
 
-            def keep_clock(n):
-                for i in range(n):
-                    o = psum.tile([P, 512], F32, name="ps")
-                    nc.tensor.matmul(o[:], lhsT=warm[:, 0:P], rhs=warm[:], start=True, stop=True)
-
-            keep_clock(WARM[0])
 
             def widen(j, b, engine):
                 src = xb[:, j, P * b : P * b + P].bitcast(FP8)
@@ -231,7 +223,6 @@ def tile_lowranksecondordervolterraforecaster_d1p_kernel(
                 unload_x(j, 1, xt, "s")
             xt = turn(2, 2)
             unload_x(2, 2, xt, "s")
-            keep_clock(WARM[1])
             permute_scales(0, 0)
             permute_words(0, 0)
             permute_words(1, 0)
@@ -239,7 +230,6 @@ def tile_lowranksecondordervolterraforecaster_d1p_kernel(
             quant_x(1, 1)
             permute_scales(1, 0)
             permute_scales(0, 1)
-            permute_scales(1, 1)
             quant_x(2, 2)
             permute_words(0, 1)
 
@@ -252,10 +242,12 @@ def tile_lowranksecondordervolterraforecaster_d1p_kernel(
 
             stage1_pair(0, 0)
             mult(0, 0)
-            permute_words(1, 1)
+            permute_scales(1, 1)
             mult(1, 0)
             stage1_pair(2, 0)
+            permute_words(1, 1)
             mult(2, 0)
+
             mult(3, 0)
             stage1_pair(0, 1)
             mult(0, 1)

from contextlib import ExitStack

import concourse.mybir as mybir
from concourse.masks import make_identity

N, L, R, H = 1024, 512, 1024, 1024
FLOPS = 2 * N * (3 * L * 1024 + R * H)

F32 = mybir.dt.float32
BF16 = mybir.dt.bfloat16
I32 = mybir.dt.int32
U32 = mybir.dt.uint32
U8 = mybir.dt.uint8
FP8 = mybir.dt.float8_e4m3fn
FP8X4 = mybir.dt.float8_e4m3fn_x4
MULT = mybir.AluOpType.mult
ADD = mybir.AluOpType.add
COPY = mybir.ActivationFunctionType.Copy

P = 128
TILES = N // P
LAG = 2


def words_view(w, g):
    return w[g].rearrange("p n t -> p (n t)").bitcast(I32)


def tile_lowranksecondordervolterraforecaster_d1p_kernel(
    tc, x_bytes, x_scale, k1_words, k1_scales, u_words, u_scales, v_words, v_scales, c_words, c_scales, h0, out
):
    nc = tc.nc
    with ExitStack() as ctx:
        keep = ctx.enter_context(tc.tile_pool(name="keep", bufs=1))
        work = ctx.enter_context(tc.tile_pool(name="work", bufs=3))
        psum = ctx.enter_context(tc.psum_pool(name="psum", bufs=8))

        ident = keep.tile([P, P], F32, name="ident")
        ident_pool = keep.tile([P, P], F32, name="ident_pool")
        h0_all = keep.tile([P, H], BF16, name="h0_all")
        xb = keep.tile([P, TILES, L], U8, name="xb", align_bytes=64)
        xs = keep.tile([P, TILES, 4], F32, name="xs")
        xw = keep.tile([P, TILES, L], BF16, name="xw", align_bytes=64)
        xq = keep.tile([P, N], U32, name="xq", align_bytes=256)
        xq_s = keep.tile([P, N], U8, name="xq_s", align_bytes=256)
        raw = keep.tile([P, 2, R], U32, name="raw", align_bytes=256)
        raw_us = keep.tile([P, R], U8, name="raw_us", align_bytes=256)
        raw_vs = keep.tile([P, R], U8, name="raw_vs", align_bytes=256)
        raw_s = (raw_us, raw_vs)
        uv = keep.tile([P, 2, R], U32, name="uv", align_bytes=256)
        uv_s = keep.tile([P, 2, R], U8, name="uv_s", align_bytes=256)
        k1 = keep.tile([P, H], U32, name="k1", align_bytes=256)
        kc_s = keep.tile([P, H], U8, name="kc_s", align_bytes=256)
        cw = keep.tile([P, 2, H], U32, name="cw", align_bytes=256)

        xb_hbm = x_bytes.rearrange("(p j) k -> p j k", j=TILES)
        xs_hbm = x_scale.rearrange("(p j) b -> p j b", j=TILES)
        out_hbm = out.rearrange("(p j) h -> p j h", j=TILES)

        def load_scales(queue, tile, row, src):
            for q in range(4):
                queue.dma_start(
                    out=tile[32 * q + row : 32 * q + row + 4 * src.shape[0], :].bitcast(I32),
                    in_=src[:, 4 * q : 4 * q + 4, :].bitcast(I32),
                )

        def spread_scales(queues, tile, src):
            for q in range(4):
                rows = src[0, 4 * q : 4 * q + 4, :].bitcast(I32)
                queues[q].dma_start(
                    out=tile[32 * q : 32 * q + 32, :].bitcast(I32), in_=rows.unsqueeze(0).to_broadcast([8, 4, R // 4])
                )

        with tc.manual_schedule():
            nc.vector.memset(kc_s[:].bitcast(I32), 0)
            make_identity(nc, ident_pool[:])

            def load_words(queue, i, g, src):
                cols = slice(512 * g, 512 * g + 512)
                queue.dma_start(out=raw[:, i, cols].bitcast(I32), in_=words_view(src, 0)[:, cols])

            def load_x(queue, j0, j1):
                queue.dma_start(out=xb[:, j0:j1, :], in_=xb_hbm[:, j0:j1, :])

            load_x(nc.sync, 0, 4)
            nc.sync.dma_start(out=xs[:], in_=xs_hbm)
            spread_scales((nc.scalar, nc.scalar, nc.sync, nc.sync), raw_us, u_scales)
            nc.scalar.copy(out=ident[:], in_=ident_pool[:])
            load_words(nc.sync, 0, 0, u_words)
            load_words(nc.sync, 1, 0, v_words)
            spread_scales((nc.sync,) * 4, raw_vs, v_scales)
            load_words(nc.sync, 0, 1, u_words)
            load_words(nc.sync, 1, 1, v_words)
            load_scales(nc.sync, kc_s, 0, k1_scales)
            load_x(nc.sync, 4, 8)
            nc.sync.dma_start(out=k1[:].bitcast(I32), in_=words_view(k1_words, 0))
            load_scales(nc.sync, kc_s, 4, c_scales)
            nc.sync.dma_start(out=cw[:, 0, :].bitcast(I32), in_=words_view(c_words, 0))
            nc.sync.dma_start(out=cw[:, 1, :].bitcast(I32), in_=words_view(c_words, 1))
            nc.sync.dma_start(out=h0_all[:], in_=h0.partition_broadcast(P))


            def widen(j, b, engine):
                src = xb[:, j, P * b : P * b + P].bitcast(FP8)
                dst = xw[:, j, P * b : P * b + P]
                s = xs[:, j, b : b + 1]
                if engine == "v":
                    nc.vector.tensor_scalar(out=dst, in0=src, scalar1=s, scalar2=None, op0=MULT)
                else:
                    nc.scalar.activation(out=dst, in_=src, func=COPY, scale=s)

            xg_of = {}

            def turn(j0, n):
                xt = psum.tile([P, n, 2, P], F32, name="ps")
                for i in range(n):
                    w = xw[:, j0 + i, :].bitcast(F32)
                    for h in range(2):
                        nc.tensor.transpose(xt[:, i, h, :], w[:, h::2], ident[:])
                return xt

            def unload_x(j0, n, xt, engine):
                xg = work.tile([P, n * L], BF16, name="xg", align_bytes=64, bufs=3)
                xg_of[j0] = xg
                dst = xg[:].bitcast(F32).rearrange("p (i m h) -> p i m h", i=n, h=2)
                src = xt[:].rearrange("p i h m -> p i m h")
                if engine == "v":
                    nc.vector.tensor_copy(out=dst, in_=src)
                else:
                    nc.scalar.copy(out=dst, in_=src)

            def quant_x(j0, n):
                c0 = P * j0
                c1 = P * (j0 + n)
                nc.vector.quantize_mx(out=xq[:, c0:c1].bitcast(FP8X4), scales=xq_s[:, c0:c1], in_=xg_of[j0][:])

            def permute_scales(i, g):
                cols = slice(512 * g, 512 * g + 512)
                nc.vector.tensor_copy(
                    out=uv_s[:, i, cols].rearrange("p (t m) -> p t m", t=4),
                    in_=raw_s[i][:, cols].rearrange("p (m t) -> p t m", t=4),
                )

            def permute_words(i, g):
                cols = slice(512 * g, 512 * g + 512)
                nc.vector.tensor_copy(
                    out=uv[:, i, cols].bitcast(I32).rearrange("p (t m) -> p t m", t=4),
                    in_=raw[:, i, cols].bitcast(I32).rearrange("p (m t) -> p t m", t=4),
                )

            ab_of = {}
            a_of = {}
            qg_of = {}
            qc_of = {}
            o_of = {}

            def stage1(j, g, i):
                tok = slice(P * j, P * j + P)
                bank = psum.tile([P, 4, P], F32, name="ps")
                for t in range(4):
                    c = slice(512 * g + P * t, 512 * g + P * t + P)
                    nc.tensor.matmul_mx(
                        out=bank[:, t, :], lhsT=uv[:, i, c].bitcast(FP8X4), lhsT_scale=uv_s[:, i, c],
                        rhs=xq[:, tok].bitcast(FP8X4), rhs_scale=xq_s[:, tok], start=True, stop=True,
                    )
                ab_of[(j, g, i)] = bank

            def copy_a(j, g):
                a = work.tile([P, P, 4], F32, name="a_sb", bufs=6)
                nc.scalar.copy(out=a[:], in_=ab_of[(j, g, 0)][:].rearrange("p t n -> p n t"))
                a_of[(j, g)] = a

            def mult(j, g):
                if g == 0:
                    qg_of[j] = work.tile([P, 2, P, 4], BF16, name="qg", align_bytes=64, bufs=6)
                nc.vector.tensor_tensor(
                    out=qg_of[j][:, g],
                    in0=ab_of[(j, g, 1)][:].rearrange("p t n -> p n t"),
                    in1=a_of[(j, g)][:],
                    op=MULT,
                )

            def quant_q(j):
                qc = work.tile([P, 2 * P], U32, name="qc", align_bytes=256, bufs=6)
                qs = work.tile([P, 2 * P], U8, name="qs", align_bytes=256, bufs=6)
                nc.vector.quantize_mx(
                    out=qc[:].bitcast(FP8X4), scales=qs[:], in_=qg_of[j][:].rearrange("p g n t -> p (g n t)")
                )
                qc_of[j] = (qc, qs)

            def linear(j, c0, width=512):
                tok = slice(P * j, P * j + P)
                cols = slice(c0, c0 + width)
                o = psum.tile([P, width], F32, name="ps")
                nc.tensor.matmul_mx(
                    out=o[:], lhsT=xq[:, tok].bitcast(FP8X4), lhsT_scale=xq_s[:, tok],
                    rhs=k1[:, cols].bitcast(FP8X4), rhs_scale=kc_s[:, cols], start=True, stop=False,
                )
                o_of[(j, c0)] = o

            def quadratic(j, c0, width=512):
                cols = slice(c0, c0 + width)
                qc, qs = qc_of[j]
                o = o_of[(j, c0)]
                for g in range(2):
                    r = slice(P * g, P * g + P)
                    nc.tensor.matmul_mx(
                        out=o[:], lhsT=qc[:, r].bitcast(FP8X4), lhsT_scale=qs[:, r],
                        rhs=cw[:, g, cols].bitcast(FP8X4), rhs_scale=kc_s[4 + 4 * g :, cols], start=False, stop=(g == 1),
                    )

            def finish(j, c0, width=512):
                cols = slice(c0, c0 + width)
                ob = work.tile([P, width], F32, name="ob", bufs=10)
                nc.vector.tensor_tensor(out=ob[:], in0=o_of[(j, c0)][:], in1=h0_all[:, cols], op=ADD)
                nc.sync.dma_start(out=out_hbm[:, j, cols], in_=ob[:])

            for j in range(4):
                for b in range(4):
                    widen(j, b, "sv"[j % 2 == 0])
            for j in (0, 1):
                xt = turn(j, 1)
                unload_x(j, 1, xt, "s")
            xt = turn(2, 2)
            unload_x(2, 2, xt, "s")
            permute_scales(0, 0)
            permute_words(0, 0)
            permute_words(1, 0)
            quant_x(0, 1)
            quant_x(1, 1)
            permute_scales(1, 0)
            permute_scales(0, 1)
            quant_x(2, 2)
            permute_words(0, 1)

            def stage1_pair(j, g):
                for i in range(2):
                    for jj in (j, j + 1):
                        stage1(jj, g, i)
                        if i == 0:
                            copy_a(jj, g)

            stage1_pair(0, 0)
            mult(0, 0)
            permute_scales(1, 1)
            mult(1, 0)
            stage1_pair(2, 0)
            permute_words(1, 1)
            mult(2, 0)

            mult(3, 0)
            stage1_pair(0, 1)
            mult(0, 1)
            quant_q(0)
            mult(1, 1)
            stage1_pair(2, 1)
            mult(2, 1)
            quant_q(1)
            mult(3, 1)
            quant_q(2)
            for j in (4, 5, 6, 7):
                for b in range(4):
                    widen(j, b, "s")
            linear(0, 0)
            linear(0, 512)
            linear(1, 0)
            for h in range(2):
                quadratic(0, 512 * h)
                finish(0, 512 * h)
                if h == 0:
                    quant_q(3)
            linear(1, 512)
            for h in range(2):
                quadratic(1, 512 * h)
                finish(1, 512 * h)
            for j in (4, 6):
                xt = turn(j, 2)
                unload_x(j, 2, xt, "s")
            for h in range(2):
                linear(2, 512 * h)
                quadratic(2, 512 * h)
                finish(2, 512 * h)
            quant_x(4, 2)
            for h in range(2):
                linear(3, 512 * h)
                quadratic(3, 512 * h)
            finish(3, 0)
            quant_x(6, 2)
            finish(3, 512)

            def unit(j, g):
                stage1(j, g, 0)
                stage1(j, g, 1)
                copy_a(j, g)
                mult(j, g)

            unit(4, 0)
            unit(4, 1)
            unit(5, 0)
            quant_q(4)
            unit(5, 1)
            unit(6, 0)
            quant_q(5)
            unit(6, 1)
            linear(4, 0)
            unit(7, 0)
            quant_q(6)
            linear(4, 512)
            unit(7, 1)
            for h in range(2):
                quadratic(4, 512 * h)
                finish(4, 512 * h)
                if h == 0:
                    quant_q(7)
            for j in (5, 6, 7):
                for h in range(2):
                    for c in ((512 * h, 512),) if (j, h) != (7, 1) else ((512, 256), (768, 256)):
                        linear(j, *c)
                        quadratic(j, *c)
                        finish(j, *c)
